import numpy as np
import ml_dtypes


def mxq(x, axis, fmt="e4m3"):
    dtype, down = {"e4m3": (ml_dtypes.float8_e4m3fn, 7), "e5m2": (ml_dtypes.float8_e5m2, 14)}[fmt]
    v = np.moveaxis(np.asarray(x, np.float32).astype(ml_dtypes.bfloat16).astype(np.float64), axis, -1)
    blocks = v.reshape(v.shape[:-1] + (-1, 32))
    amax = np.abs(blocks).max(-1, keepdims=True)
    byte = np.maximum(np.where(amax > 0, np.frexp(amax)[1] - 1 + 127, 0) - down, 1)
    scale = np.exp2(byte - 127.0)
    codes = (blocks / scale).astype(np.float32).astype(dtype).astype(np.float64)
    return np.moveaxis((codes * scale).reshape(v.shape), -1, axis)


WIDE = False


def mx_kscale(k):
    if not WIDE:
        return np.ones(k)
    levels = np.array([10, -10, 5, -5, 0])
    if k % 512:
        return np.exp2(np.random.permutation(np.resize(levels, k // 32))).repeat(32)
    a = np.empty((k // 512, 16))
    for p in range(k // 512):
        a[p, :8] = np.random.permutation(np.resize(levels, 8))
        for g in range(8):
            far = levels[np.abs(levels - a[p, g]) >= 10]
            a[p, g + 8] = far[np.random.randint(len(far))]
    return np.exp2(a.ravel()).repeat(32)


BF16 = ml_dtypes.bfloat16


def bf(x):
    return np.asarray(x, np.float32).astype(BF16)


def f64(x):
    return np.asarray(x).astype(np.float64)


M, N, D, R, F, H = 3, 1024, 512, 4, 512, 1024
RF = R * F


def draw0():
    s = mx_kscale(D)
    t = mx_kscale(F)
    return {
        "x": bf(np.random.standard_normal((M, N, D)) * s),
        "w": bf(np.random.standard_normal((M, D, RF)) / np.sqrt(D) / s[:, None]),
        "b": bf(0.5 * np.random.standard_normal((M, RF))),
        "omega": bf((0.5 + 0.1 * np.random.standard_normal((R, F))) * t[None, :]),
        "wo": bf(np.random.standard_normal((F, H)) / np.sqrt(F) / t[:, None]),
        "bo": bf(0.3 * np.random.standard_normal(H)),
    }


def project_modalities(x, w, b):
    h = mxq(x, 2, "e4m3") @ mxq(w, 1, "e4m3")
    return h + b[:, None, :]


def fuse_ranks(h, omega):
    p = h[0] * h[1] * h[2]
    p = p.reshape(p.shape[0], omega.shape[0], omega.shape[1])
    return np.sum(omega[None, :, :] * p, axis=1)


def core(x, w, b, omega, wo, bo):
    h = project_modalities(f64(x), f64(w), f64(b))
    z = fuse_ranks(h, f64(omega))
    y = (mxq(z, 1, "e4m3") @ mxq(f64(wo), 0, "e4m3")) + f64(bo)[None, :]
    return y


def e4m3fn_bytes(y):
    return np.clip(np.asarray(y, np.float64), -448.0, 448.0).astype(np.float32).astype(ml_dtypes.float8_e4m3fn).view(np.uint8)


def e4m3fn_values(b):
    return np.asarray(b, np.uint8).view(ml_dtypes.float8_e4m3fn).astype(np.float64)


def setup_inputs():
    d = draw0()
    x0 = np.asarray(d['w']).astype(np.float64)
    s = (np.max(np.abs(x0), axis=(0, 2), keepdims=True) / 448.0).astype(np.float32)
    out = {}
    for k, v in d.items():
        if k == 'w':
            out['w_bytes'] = e4m3fn_bytes(x0 / s.astype(np.float64))
            out['w_scale'] = s
        else:
            out[k] = v
    return out


def reference(x, w_bytes, w_scale, b, omega, wo, bo):
    return core(x, e4m3fn_values(w_bytes) * w_scale.astype(np.float64), b, omega, wo, bo)

from contextlib import ExitStack

import concourse.mybir as mybir
from concourse.masks import make_identity

F32 = mybir.dt.float32
BF16 = mybir.dt.bfloat16
U32 = mybir.dt.uint32
U8 = mybir.dt.uint8
FP8 = mybir.dt.float8_e4m3fn
FP8X4 = mybir.dt.float8_e4m3fn_x4
ACT = mybir.ActivationFunctionType
ALU = mybir.AluOpType

M, N, D, R, F, H = 3, 1024, 512, 4, 512, 1024
FLOPS = 2 * M * N * D * R * F + 2 * N * F * H

P = 128
HALF = 512


def tile_lowranktrimodalfusion_kernel(tc, x, w_bytes, w_scale, b, omega, wo, bo, out):
    nc = tc.nc
    with ExitStack() as ctx:
        keep = ctx.enter_context(tc.tile_pool(name="keep", bufs=1))
        stage = ctx.enter_context(tc.tile_pool(name="stage", bufs=3))
        psum = ctx.enter_context(tc.psum_pool(name="psum", bufs=1))
        ctx.enter_context(tc.manual_schedule())

        ws = keep.tile([P, 4], F32, name="ws")
        vec = keep.tile([P, F], BF16, name="vec")
        nc.gpsimd.memset(vec[:], 0.0)
        ident = keep.tile([P, P], F32, name="ident")
        make_identity(nc, ident[:])

        nc.scalar.dma_start(out=ws[:], in_=w_scale.rearrange("a (p j) o -> p (a j o)", j=4))
        nc.scalar.dma_start(out=vec[0:12, :], in_=b.rearrange("m (r f) -> (m r) f", r=R))
        nc.scalar.dma_start(out=vec[12:16, :], in_=omega)

        w_first, w_rest, xr = [], [], {}
        for m in range(M):
            t0 = keep.tile([P, 4, F], U8, name="w_first%d" % m)
            w_first.append(t0)
            t1 = keep.tile([P, 4, 3 * F], U8, name="w_rest%d" % m)
            w_rest.append(t1)
            for half in range(2):
                t2 = keep.tile([P, 4, D], BF16, name="xr%d%d" % (m, half))
                xr[m, half] = t2
        wo_raw = keep.tile([P, 4, H], BF16, name="wo_raw")
        bo_sb = keep.tile([P, H], BF16, name="bo_sb")

        def load_x(m, half):
            src = x[m].rearrange("(p a) k -> p a k", a=8)
            nc.sync.dma_start(out=xr[m, half][:], in_=src[:, 4 * half : 4 * half + 4, :])

        for m in range(M):
            src = w_bytes[m].rearrange("(p j) n -> p j n", j=4)
            nc.sync.dma_start(out=w_first[m][:], in_=src[:, :, 0:F])
            load_x(m, 0)
        for m in range(M):
            src = w_bytes[m].rearrange("(p j) n -> p j n", j=4)
            nc.sync.dma_start(out=w_rest[m][:], in_=src[:, :, F:])
        for m in range(M):
            load_x(m, 1)
        wo_rows = wo.rearrange("(g t i) n -> t g i n", t=4, i=4)
        for t in range(4):
            nc.sync.dma_start(out=wo_raw[:, t, :], in_=wo_rows[t])
        nc.sync.dma_start(out=bo_sb[:], in_=bo.partition_broadcast(P))

        xc, xs, wc, wsc = {}, {}, {}, {}
        for m in range(M):
            for half in range(2):
                c = keep.tile([P, HALF], U32, name="xc%d%d" % (m, half), align_bytes=64)
                s = keep.tile([P, HALF], U8, name="xs%d%d" % (m, half), align_bytes=64)
                xc[m, half], xs[m, half] = c, s
            for r in range(R):
                c = keep.tile([P, F], U32, name="wc%d%d" % (m, r), align_bytes=64)
                s = keep.tile([P, F], U8, name="wsc%d%d" % (m, r), align_bytes=64)
                wc[m, r], wsc[m, r] = c, s
        woc = keep.tile([P, H], U32, name="woc", align_bytes=64)
        wos = keep.tile([P, H], U8, name="wos", align_bytes=64)
        wog = keep.tile([P, H, 4], BF16, name="wog", align_bytes=64)
        zacc = {}
        for t in range(4):
            z = keep.tile([P, HALF], F32, name="zacc%d" % t)
            zacc[1, t] = z
        zb, zg, zc, zs = {}, {}, {}, {}
        for half in range(2):
            t0 = keep.tile([P, 4, HALF], BF16, name="zb%d" % half)
            t1 = keep.tile([P, HALF, 4], BF16, name="zg%d" % half, align_bytes=64)
            t2 = keep.tile([P, HALF], U32, name="zc%d" % half, align_bytes=64)
            t3 = keep.tile([P, HALF], U8, name="zs%d" % half, align_bytes=64)
            zb[half], zg[half], zc[half], zs[half] = t0, t1, t2, t3

        xt_of, xg_of = {}, {}

        def x_turn(m, half, pair):
            if pair == 0:
                g = stage.tile([P, HALF, 4], BF16, name="xg", align_bytes=64)
                xg_of[m, half] = g
            xt = psum.tile([P, 2, 2, P], F32, name="aux" if half else ("h%d" if pair == 0 else "z%d") % m)
            words = xr[m, half][:].rearrange("p a k -> p (a k)").bitcast(F32)
            for i in range(2):
                a = 2 * pair + i
                for u in range(2):
                    nc.tensor.transpose(xt[:, i, u, :], words[:, a * 256 + u : (a + 1) * 256 : 2], ident[:])
            xt_of[m, half, pair] = xt

        def x_out(m, half, pair, on_scalar):
            dst = xg_of[m, half][:].rearrange("p n j -> p (n j)").bitcast(F32)
            dst = dst[:, pair * 512 : (pair + 1) * 512].rearrange("p (a r u) -> p a r u", a=2, u=2)
            src = xt_of[m, half, pair][:].rearrange("p a u r -> p a r u")
            if on_scalar:
                nc.scalar.copy(out=dst, in_=src)
            else:
                nc.vector.tensor_copy(out=dst, in_=src)

        def x_quant(m, half):
            nc.vector.quantize_mx(
                out=xc[m, half][:].bitcast(FP8X4),
                scales=xs[m, half][:],
                in_=xg_of[m, half][:].rearrange("p n j -> p (n j)"),
            )

        wb_of, wg_of = {}, {}

        def w_widen(m, r, j, on_scalar=True):
            if j == 0:
                t0 = stage.tile([P, 4, F], BF16, name="wb")
                wb_of[m, r] = t0
            src = w_first[m][:, j, :] if r == 0 else w_rest[m][:, j, (r - 1) * F : r * F]
            if on_scalar:
                nc.scalar.activation(
                    out=wb_of[m, r][:, j, :], in_=src.bitcast(FP8), func=ACT.Copy, scale=ws[:, j : j + 1]
                )
            else:
                nc.vector.tensor_scalar(
                    out=wb_of[m, r][:, j, :], in0=src.bitcast(FP8), scalar1=ws[:, j : j + 1], scalar2=None, op0=ALU.mult
                )

        def w_weave(m, r, part):
            if part == 0:
                t0 = stage.tile([P, F, 4], BF16, name="wg", align_bytes=64)
                wg_of[m, r] = t0
            dst = wg_of[m, r][:].rearrange("p (t g i) j -> p g t j i", t=4, i=4)
            src = wb_of[m, r][:].rearrange("p j (g t i) -> p g t j i", t=4, i=4)
            gs = slice(part * 16, part * 16 + 16)
            nc.vector.tensor_copy(out=dst[:, gs], in_=src[:, gs])

        def w_quant(m, r):
            nc.vector.quantize_mx(
                out=wc[m, r][:].bitcast(FP8X4),
                scales=wsc[m, r][:],
                in_=wg_of[m, r][:].rearrange("p n j -> p (n j)"),
            )

        def wo_weave(part):
            cs = slice(part * 512, part * 512 + 512)
            dst = wog[:, cs, :].rearrange("p (c i) t -> p c t i", i=4)
            src = wo_raw[:, :, cs].rearrange("p t (c i) -> p c t i", i=4)
            nc.vector.tensor_copy(out=dst, in_=src)

        def wo_quant(part):
            cs = slice(part * 512, part * 512 + 512)
            nc.vector.quantize_mx(
                out=woc[:, cs].bitcast(FP8X4),
                scales=wos[:, cs],
                in_=wog[:, cs, :].rearrange("p n j -> p (n j)"),
            )

        ident_bf = keep.tile([P, P], BF16, name="ident_bf")
        vecp = keep.tile([P, 4, P], BF16, name="vecp")
        cols = keep.tile([P, 4, 16], F32, name="cols")
        ob0 = keep.tile([P, 4, 4], F32, name="ob0")

        def columns_a():
            nc.vector.tensor_copy(out=ident_bf[:], in_=ident[:])
            nc.vector.tensor_copy(
                out=vecp[:].rearrange("p t (g i) -> p t g i", i=4),
                in_=vec[:].rearrange("p (g t i) -> p t g i", t=4, i=4),
            )

        def columns_b():
            vt = psum.tile([P, 4, P], BF16, name="aux")
            for t in range(4):
                nc.tensor.transpose(vt[:, t, :], vecp[:, t, :], ident_bf[:])
            nc.vector.tensor_copy(out=cols[:], in_=vt[:, :, 0:16])

        def columns_c():
            nc.vector.tensor_tensor(out=ob0[:], in0=cols[:, :, 12:16], in1=cols[:, :, 0:4], op=ALU.mult)

        units = [(0, r, t, 0, 512, "v") for r in range(R) for t in range(4)]
        units += [(1, r, t, 0, 512, "g" if t % 2 else "v") for r in range(R - 1) for t in range(4)]
        units += [(1, R - 1, t, c, 256, "v") for c in (0, 256) for t in range(4)]
        zps = {}
        hps, a_of, b_of, ab_of, pr_of = {}, {}, {}, {}, {}

        def mm(u, m):
            half, r, t, c0, w, mode = units[u]
            h = psum.tile([P, 512], F32, name=("z%d" if u >= 21 and u % 2 else "h%d") % m)
            hps[u, m] = h
            nc.tensor.matmul_mx(
                out=h[:, 0:w],
                lhsT=wc[m, r][:, t * P : (t + 1) * P].bitcast(FP8X4),
                lhsT_scale=wsc[m, r][:, t * P : (t + 1) * P],
                rhs=xc[m, half][:, c0 : c0 + w].bitcast(FP8X4),
                rhs_scale=xs[m, half][:, c0 : c0 + w],
                start=True,
                stop=True,
            )

        def first_factor(u):
            half, r, t, c0, w, mode = units[u]
            a = stage.tile([P, 512], F32, name="a")
            a_of[u] = a
            nc.scalar.activation(
                out=a[:, 0:w],
                in_=hps[u, 0][:, 0:w],
                func=ACT.Identity,
                scale=cols[:, t, 12 + r : 13 + r],
                bias=ob0[:, t, r : r + 1],
            )

        def second_on_scalar(u):
            half, r, t, c0, w, mode = units[u]
            bb = stage.tile([P, 512], F32, name="bb")
            b_of[u] = bb
            nc.scalar.activation(
                out=bb[:, 0:w], in_=hps[u, 1][:, 0:w], func=ACT.Identity, bias=cols[:, t, 4 + r : 5 + r]
            )

        def product_on_gpsimd(u):
            half, r, t, c0, w, mode = units[u]
            ab = stage.tile([P, 512], F32, name="ab")
            ab_of[u] = ab
            nc.gpsimd.tensor_tensor(out=ab[:, 0:w], in0=a_of[u][:, 0:w], in1=b_of[u][:, 0:w], op=ALU.mult)

        def second_factor(u):
            half, r, t, c0, w, mode = units[u]
            ab = stage.tile([P, 512], F32, name="ab")
            ab_of[u] = ab
            nc.vector.scalar_tensor_tensor(
                out=ab[:, 0:w], in0=hps[u, 1][:, 0:w], scalar=cols[:, t, 4 + r : 5 + r], in1=a_of[u][:, 0:w],
                op0=ALU.add, op1=ALU.mult,
            )

        def third_factor(u):
            half, r, t, c0, w, mode = units[u]
            if half == 1 and r == 0:
                dst = zacc[half, t][:, c0 : c0 + w]
            else:
                pr = stage.tile([P, 512], F32, name="pr")
                pr_of[u] = pr
                dst = pr[:, 0:w]
            nc.vector.scalar_tensor_tensor(
                out=dst, in0=hps[u, 2][:, 0:w], scalar=cols[:, t, 8 + r : 9 + r], in1=ab_of[u][:, 0:w],
                op0=ALU.add, op1=ALU.mult,
            )

        def rank_sum(u, eng):
            half, r, t, c0, w, mode = units[u]
            if half == 0:
                if r == 0:
                    z_bank = psum.tile([P, 512], F32, name="z%d" % t)
                    zps[t] = z_bank
                nc.tensor.matmul(zps[t][:], lhsT=ident[:], rhs=pr_of[u][:], start=r == 0, stop=r == R - 1)
                return
            if r == 0:
                return
            z = zacc[half, t][:, c0 : c0 + w]
            dst = z if r < R - 1 else zb[half][:, t, c0 : c0 + w]
            eng.tensor_tensor(out=dst, in0=z, in1=pr_of[u][:, 0:w], op=ALU.add)

        def z_out(t):
            nc.scalar.copy(out=zb[0][:, t, :], in_=zps[t][:])

        def z_weave(half, c0, w):
            dst = zg[half][:, c0 : c0 + w, :].rearrange("p (c i) t -> p c t i", i=4)
            src = zb[half][:, :, c0 : c0 + w].rearrange("p t (c i) -> p c t i", i=4)
            nc.vector.tensor_copy(out=dst, in_=src)

        def z_quant(half, c0, w):
            nc.vector.quantize_mx(
                out=zc[half][:, c0 : c0 + w].bitcast(FP8X4),
                scales=zs[half][:, c0 : c0 + w],
                in_=zg[half][:, c0 : c0 + w, :].rearrange("p n j -> p (n j)"),
            )

        out_rows = out.rearrange("(p a) h -> p a h", a=8)
        osb_of, y_of = {}, {}

        def out_mm(half, a, hh):
            y = psum.tile([P, 512], F32, name="aux" if hh else "z3")
            hs = slice(hh * 512, hh * 512 + 512)
            ts = slice(a * P, (a + 1) * P)
            nc.tensor.matmul_mx(
                out=y[:],
                lhsT=zc[half][:, ts].bitcast(FP8X4),
                lhsT_scale=zs[half][:, ts],
                rhs=woc[:, hs].bitcast(FP8X4),
                rhs_scale=wos[:, hs],
                start=True,
                stop=True,
            )
            y_of[half, a, hh] = y

        def out_tile(half, a, hh):
            y = y_of[half, a, hh]
            if hh == 0:
                o = stage.tile([P, H], F32, name="o")
                osb_of[half, a] = o
            hs = slice(hh * 512, hh * 512 + 512)
            nc.vector.tensor_tensor(out=osb_of[half, a][:, hs], in0=y[:], in1=bo_sb[:, hs], op=ALU.add)
            if hh == 1:
                nc.sync.dma_start(out=out_rows[:, 4 * half + a, :], in_=osb_of[half, a][:])

        v_tasks, s_tasks, t_tasks = {}, {}, {}

        def at(table, step, fn, *args):
            table.setdefault(step, []).append((fn, args))

        def go(tasks):
            for fn, args in tasks:
                fn(*args)

        for m in range(M):
            x_turn(m, 0, 0)
            x_turn(m, 0, 1)
        for j in range(4):
            w_widen(0, 0, j)
        x_out(0, 0, 0, False)
        x_out(0, 0, 1, False)
        x_out(1, 0, 0, False)
        x_quant(0, 0)
        w_weave(0, 0, 0)
        w_weave(0, 0, 1)
        for j in range(4):
            w_widen(1, 0, j)
        x_out(1, 0, 1, False)
        w_quant(0, 0)
        x_out(2, 0, 0, True)
        columns_a()
        columns_b()
        x_quant(1, 0)
        w_weave(1, 0, 0)
        w_weave(1, 0, 1)
        columns_c()
        x_out(2, 0, 1, True)
        for j in range(4):
            w_widen(2, 0, j)
        w_quant(1, 0)
        x_quant(2, 0)
        w_weave(2, 0, 0)
        w_weave(2, 0, 1)
        w_quant(2, 0)

        for r in range(1, R):
            base = 4 * r - 8
            for i in range(12):
                at(s_tasks, max(base + i // 3, -2), w_widen, i // 4, r, i % 4)
            seq = []
            for m in range(M):
                seq += [(w_weave, m, r, 0), (w_weave, m, r, 1)]
                if m:
                    seq.insert(len(seq) - 1, (w_quant, m - 1, r))
            seq.append((w_quant, M - 1, r))
            for i, task in enumerate(seq):
                at(v_tasks, max(base + 2 + i * 4 // 9, -1), *task)
        for m in range(M):
            for pair in range(2):
                at(t_tasks, 7 + 2 * m + pair, x_turn, m, 1, pair)
                at(s_tasks, 8 + 2 * m + pair, x_out, m, 1, pair, True)
            at(v_tasks, 10 + 2 * m - (m == 2), x_quant, m, 1)
        for t in range(4):
            at(s_tasks, 16 + t // 2, z_out, t)
        for part in range(2):
            at(v_tasks, 14 + 2 * part, wo_weave, part)
            at(v_tasks, 15 + 2 * part, wo_quant, part)
        at(v_tasks, 18, z_weave, 0, 0, 512)
        at(v_tasks, 19, z_quant, 0, 0, 512)
        for a in range(4):
            for hh in range(2):
                at(t_tasks, 19 + 2 * a + hh, out_mm, 0, a, hh)
                at(v_tasks, 20 + 2 * a + hh, out_tile, 0, a, hh)
        last = len(units) - 1
        at(v_tasks, last - 2, z_weave, 1, 0, 256)
        at(v_tasks, last - 1, z_quant, 1, 0, 256)
        for a in range(2):
            for hh in range(2):
                at(t_tasks, last - 1 + a, out_mm, 1, a, hh)
                at(v_tasks, last + a, out_tile, 1, a, hh)
        at(v_tasks, last + 1, z_weave, 1, 256, 256)
        at(v_tasks, last + 1, z_quant, 1, 256, 256)
        for a in range(2, 4):
            for hh in range(2):
                at(t_tasks, last + 2 + 2 * a + hh, out_mm, 1, a, hh)
                at(v_tasks, last + 3 + 2 * a + hh, out_tile, 1, a, hh)

        mm(0, 0)
        for s in range(-2, last + 14):
            if 0 <= s + 2 <= last:
                first_factor(s + 2)
                mm(s + 2, 1)
                if units[s + 2][5] == "g":
                    second_on_scalar(s + 2)
            if 0 <= s + 1 <= last:
                if units[s + 1][5] == "g":
                    product_on_gpsimd(s + 1)
                else:
                    second_factor(s + 1)
                mm(s + 1, 2)
            if s + 3 <= last:
                mm(s + 3, 0)
            if 0 <= s <= last:
                third_factor(s)
            go(s_tasks.get(s, []))
            go(v_tasks.get(s, []))
            go(t_tasks.get(s, []))
            if 0 <= s <= last:
                rank_sum(s, nc.vector if s > last - 2 else nc.gpsimd)
